import numpy as np
import ml_dtypes


def mxq(x, axis, fmt="e4m3"):
    dtype, down = {"e4m3": (ml_dtypes.float8_e4m3fn, 7), "e5m2": (ml_dtypes.float8_e5m2, 14)}[fmt]
    v = np.moveaxis(np.asarray(x, np.float32).astype(ml_dtypes.bfloat16).astype(np.float64), axis, -1)
    blocks = v.reshape(v.shape[:-1] + (-1, 32))
    amax = np.abs(blocks).max(-1, keepdims=True)
    byte = np.maximum(np.where(amax > 0, np.frexp(amax)[1] - 1 + 127, 0) - down, 1)
    scale = np.exp2(byte - 127.0)
    codes = (blocks / scale).astype(np.float32).astype(dtype).astype(np.float64)
    return np.moveaxis((codes * scale).reshape(v.shape), -1, axis)


WIDE = False


def mx_kscale(k):
    if not WIDE:
        return np.ones(k)
    levels = np.array([10, -10, 5, -5, 0])
    if k % 512:
        return np.exp2(np.random.permutation(np.resize(levels, k // 32))).repeat(32)
    a = np.empty((k // 512, 16))
    for p in range(k // 512):
        a[p, :8] = np.random.permutation(np.resize(levels, 8))
        for g in range(8):
            far = levels[np.abs(levels - a[p, g]) >= 10]
            a[p, g + 8] = far[np.random.randint(len(far))]
    return np.exp2(a.ravel()).repeat(32)


def f64(x):
    return np.asarray(x).astype(np.float64)


def striped(idx):
    return np.tile(np.asarray(idx).reshape(-1, 16).T, (8, 1)).astype(np.uint16)


def unstriped(offs):
    return offs[:16].T.reshape(-1).astype(np.int64)


E2M1 = np.array([0.0, 0.5, 1.0, 1.5, 2.0, 3.0, 4.0, 6.0, -0.0, -0.5, -1.0, -1.5, -2.0, -3.0, -4.0, -6.0])


def pack_weight(w, fmt):
    k, n = w.shape
    w = f64(np.asarray(w, np.float32).astype(ml_dtypes.bfloat16)).reshape(k // 32, 32, n)
    amax = np.abs(w).max(1)
    if fmt == "e4m3":
        byte = np.frexp(amax)[1] - 1 + 127 - 7
    else:
        mant, ex = np.frexp(amax / 6.0)
        byte = np.where(mant > 0.5, ex, ex - 1) + 127
    byte = np.clip(np.where(amax > 0, byte, 1), 1, 254)
    scaled = (w * np.exp2(127.0 - byte)[:, None, :]).reshape(k, n).astype(np.float32)
    by_word = np.ascontiguousarray(scaled.reshape(k // 512, 128, 4, n).transpose(0, 1, 3, 2))
    if fmt == "e4m3":
        words = by_word.astype(ml_dtypes.float8_e4m3fn).view(np.uint8)
    else:
        c = by_word.astype(ml_dtypes.float4_e2m1fn).view(np.uint8) & 0xF
        words = (c[..., 0::2] | (c[..., 1::2] << 4)).reshape(k // 512, 128, 2 * n)
    return np.ascontiguousarray(words), np.ascontiguousarray(byte.astype(np.uint8).reshape(k // 512, 16, n))


def unpack_weight(words, scales, fmt):
    g, _, n = scales.shape
    words = np.ascontiguousarray(words).reshape(g, 128, n, -1)
    if fmt == "e4m3":
        vals = words.view(ml_dtypes.float8_e4m3fn).astype(np.float64)
    else:
        nib = np.empty((g, 128, n, 4), np.uint8)
        nib[..., 0::2] = words & 0xF
        nib[..., 1::2] = words >> 4
        vals = E2M1[nib]
    vals = vals * np.repeat(np.exp2(scales.astype(np.float64) - 127.0), 8, axis=1)[..., None]
    return vals.transpose(0, 1, 3, 2).reshape(g * 512, n)


D, E, T, I, Q = 512, 512, 2048, 512, 128


def setup_inputs():
    n = np.random.standard_normal
    idx2 = np.random.permutation(I)[:I]
    idx = np.random.permutation(T)[:I]
    fd = mx_kscale(D)
    fe = mx_kscale(E)
    keysp = pack_weight(n((D, T)) / fd[:, None], "e4m3")
    valsp = pack_weight(n((E, T)) / fe[:, None], "e4m3")
    return {
        "query": (n((D, Q)) * 0.8 / np.sqrt(D) * fd[:, None]).astype(np.float32),
        "keys_words": keysp[0],
        "keys_scales": keysp[1],
        "reserve": (np.random.uniform(0.5, 2.0, (Q, 1))).astype(np.float32),
        "gout": (n((E, Q)) * 1 / np.sqrt(E) * fe[:, None]).astype(np.float32),
        "vals_words": valsp[0],
        "vals_scales": valsp[1],
        "old": (0.5 * n((Q, T))).astype(np.float32),
        "offs2": striped(idx2),
        "offs": striped(idx),
    }


def reference(query, keys_words, keys_scales, reserve, gout, vals_words, vals_scales, old, offs2, offs):
    idx2 = unstriped(offs2)
    idx = unstriped(offs)
    keysu = unpack_weight(keys_words, keys_scales, "e4m3")
    valsu = unpack_weight(vals_words, vals_scales, "e4m3")
    queryq = mxq(f64(query), 0, "e4m3")
    keysidxg = keysu[:, idx]
    a = queryq.T @ keysidxg
    p = np.exp(a)
    z = np.sum(p, axis=1, keepdims=True)
    r = p / (p + p[:, idx2] + f64(reserve))
    goutq = mxq(f64(gout), 0, "e4m3")
    valsidxg = valsu[:, idx]
    c0 = goutq.T @ valsidxg
    dr = c0 * p / z
    dz = np.sum(c0 * r * p / np.square(z) * (-1.0), axis=1, keepdims=True)
    e1 = dr * p / np.square(p + p[:, idx2] + f64(reserve)) * (-1.0)
    s1 = np.zeros((Q, I))
    s1[:, idx2] = e1
    dp = c0 * r / z + dr / (p + p[:, idx2] + f64(reserve)) + dz + s1 - dr * p / np.square(p + p[:, idx2] + f64(reserve))
    da = dp * p
    gs = da * 512.0
    gf = np.zeros((Q, T))
    gf[:, idx] = gs
    y = f64(old) + gf
    return y

@@ -1,0 +1,157 @@
+from contextlib import ExitStack
+
+import concourse.mybir as mybir
+
+D, E, T, I, Q = 512, 512, 2048, 512, 128
+FLOPS = 2 * Q * I * (D + E)
+
+F32 = mybir.dt.float32
+BF16 = mybir.dt.bfloat16
+I32 = mybir.dt.int32
+U32 = mybir.dt.uint32
+U16 = mybir.dt.uint16
+U8 = mybir.dt.uint8
+FP8X4 = mybir.dt.float8_e4m3fn_x4
+ALU = mybir.AluOpType
+ACT = mybir.ActivationFunctionType
+
+P = 128
+PACK = 4
+H = I // 2
+LIST_COLS = I // 16
+SHARE_COLS = 768
+VAL_PLANE = 4
+OUT_CHUNKS = (512, 512, 512, 256, 256)
+
+
+def tile_attend_bneighbourshare_s_kernel(tc, query, keys_words, keys_scales, reserve, gout, vals_words, vals_scales, old, offs2, offs, out):
+    nc = tc.nc
+    with ExitStack() as ctx:
+        lists = ctx.enter_context(tc.tile_pool(name="lists", bufs=1))
+        sb = ctx.enter_context(tc.tile_pool(name="sb", bufs=1))
+        psum = ctx.enter_context(tc.psum_pool(name="psum", bufs=1))
+
+        halves = [slice(h * H, (h + 1) * H) for h in range(2)]
+        list_halves = [slice(h * LIST_COLS // 2, (h + 1) * LIST_COLS // 2) for h in range(2)]
+
+        tokens = lists.tile([P, LIST_COLS], U16, name="tokens")
+        links = lists.tile([P, LIST_COLS], U16, name="links")
+        nc.sync.dma_start(tokens[:], offs)
+        nc.sync.dma_start(links[:], offs2)
+
+        q_raw = sb.tile([P, PACK, Q], F32, name="q_raw", tag="staged", align_bytes=64)
+        nc.scalar.dma_start(out=q_raw[:], in_=query.rearrange("(p j) w -> p j w", j=PACK))
+        k_pool = sb.tile([P, T], I32, name="k_pool", tag="keys_then_scales", align_bytes=64)
+        nc.scalar.dma_start(out=k_pool[:], in_=keys_words[0].rearrange("p n t -> p (n t)").bitcast(I32))
+        g_raw = sb.tile([P, PACK, Q], F32, name="g_raw", align_bytes=64)
+        nc.scalar.dma_start(out=g_raw[:], in_=gout.rearrange("(p j) w -> p j w", j=PACK))
+
+        def load_scales(name, scales, first, queues):
+            plane = sb.tile([P, T], U8, name=name, align_bytes=64)
+            words = plane[:].bitcast(I32)
+            nc.vector.memset(words, 0)
+            rows = scales[0].bitcast(I32)
+            for quad in range(4):
+                queues[quad].dma_start(out=words[32 * quad + first : 32 * quad + first + 4, :], in_=rows[4 * quad : 4 * quad + 4, :])
+            return plane
+
+        ks_pool = load_scales("ks_pool", keys_scales, 0, [nc.sync] * 4)
+        vs_pool = load_scales("vs_pool", vals_scales, VAL_PLANE, [nc.gpsimd, nc.gpsimd, nc.sync, nc.sync])
+        res = sb.tile([P, 1], F32, name="res")
+        nc.gpsimd.dma_start(out=res[:], in_=reserve)
+
+        gf = sb.tile([P, T], F32, name="gf")
+        nc.vector.memset(gf[:, : T // 2 + 1], 0.0)
+        nc.vector.memset(gf[:, T // 2 + 1 :], 0.0)
+
+        def interleave(name, raw):
+            grouped = sb.tile([P, Q, PACK], BF16, name=name, align_bytes=64)
+            nc.scalar.copy(out=grouped[:], in_=raw[:].rearrange("p j w -> p w j"))
+            return grouped
+
+        def quantize(name, grouped):
+            codes = sb.tile([P, Q], U32, name=name + "_codes", align_bytes=64)
+            scales = sb.tile([P, Q], U8, name=name + "_scales", align_bytes=64)
+            nc.vector.quantize_mx(out=codes[:].bitcast(FP8X4), scales=scales[:], in_=grouped[:].rearrange("p w j -> p (w j)"))
+            return codes, scales
+
+        def gather_scales(name, plane, tag):
+            picked = sb.tile([P, I], U8, name=name, tag=tag, align_bytes=64)
+            nc.vector.tensor_copy(picked[:], plane[:].indirect(tokens[:]))
+            return picked
+
+        def products(name, pool_words, picked_scales, first, codes, scales):
+            banks = []
+            for h in range(2):
+                picked = sb.tile([P, H], U32, name=name + "_words%d" % h, align_bytes=64)
+                nc.vector.tensor_copy(picked[:], pool_words[:].bitcast(U32).indirect(tokens[:, list_halves[h]]))
+                bank = psum.tile([P, H], F32, name=name + "_bank%d" % h)
+                nc.tensor.matmul_mx(
+                    out=bank[:], lhsT=codes[:].bitcast(FP8X4), lhsT_scale=scales[:],
+                    rhs=picked[:].bitcast(FP8X4), rhs_scale=picked_scales[first:P, halves[h]],
+                    start=True, stop=True,
+                )
+                banks.append(bank)
+            return banks
+
+        q_grouped = interleave("q_grouped", q_raw)
+        v_pool = sb.tile([P, T], I32, name="v_pool", tag="staged", align_bytes=64)
+        nc.scalar.dma_start(out=v_pool[:], in_=vals_words[0].rearrange("p n t -> p (n t)").bitcast(I32))
+        ks = gather_scales("ks", ks_pool, "ks")
+        q_codes, q_scales = quantize("q", q_grouped)
+        a = products("a", k_pool, ks, 0, q_codes, q_scales)
+
+        p = sb.tile([P, I], F32, name="p")
+        z_part = [sb.tile([P, 1], F32, name="z_part%d" % h) for h in range(2)]
+        for h in range(2):
+            nc.scalar.activation(out=p[:, halves[h]], in_=a[h][:], func=ACT.Exp, accum_out=z_part[h][:])
+        g_grouped = interleave("g_grouped", g_raw)
+        vs = gather_scales("vs", vs_pool, "keys_then_scales")
+
+        linked = sb.tile([P, I], F32, name="linked")
+        den = sb.tile([P, I], F32, name="den")
+        root = sb.tile([P, I], F32, name="root")
+        inv = sb.tile([P, I], F32, name="inv")
+        for h in range(2):
+            nc.vector.tensor_copy(linked[:, halves[h]], p[:].indirect(links[:, list_halves[h]]))
+        for h in range(2):
+            nc.vector.scalar_tensor_tensor(out=den[:, halves[h]], in0=linked[:, halves[h]], scalar=res[:], in1=p[:, halves[h]], op0=ALU.add, op1=ALU.add)
+            nc.scalar.activation(out=root[:, halves[h]], in_=den[:, halves[h]], func=ACT.Abs_reciprocal_sqrt)
+            nc.scalar.activation(out=inv[:, halves[h]], in_=root[:, halves[h]], func=ACT.Square)
+        z_root = sb.tile([P, 1], F32, name="z_root")
+        z_inv = sb.tile([P, 1], F32, name="z_inv")
+        share = sb.tile([P, I], F32, name="share")
+        nc.scalar.activation(out=z_root[:], in_=z_part[0][:], func=ACT.Abs_reciprocal_sqrt, bias=z_part[1][:])
+        nc.scalar.activation(out=z_inv[:], in_=z_root[:], func=ACT.Square)
+        nc.scalar.activation(out=share[:], in_=p[:], func=ACT.Copy, scale=z_inv[:])
+
+        g_codes, g_scales = quantize("g", g_grouped)
+        c0 = products("c0", v_pool, vs, VAL_PLANE, g_codes, g_scales)
+        before = sb.tile([P, T], F32, name="before", tag="staged", align_bytes=64)
+        nc.sync.dma_start(out=before[:], in_=old)
+
+        r = sb.tile([P, I], F32, name="r")
+        v = sb.tile([P, I], F32, name="v")
+        for h in range(2):
+            nc.vector.tensor_tensor(out=r[:, halves[h]], in0=p[:, halves[h]], in1=inv[:, halves[h]], op=ALU.mult)
+        for h in range(2):
+            nc.vector.scalar_tensor_tensor(out=v[:, halves[h]], in0=c0[h][:], scalar=-512.0, in1=r[:, halves[h]], op0=ALU.mult, op1=ALU.mult)
+        weighed = sb.tile([P, I], F32, name="weighed")
+        through_z = sb.tile([P, 1], F32, name="through_z")
+        own = sb.tile([P, I], F32, name="own")
+        shared = sb.tile([P, SHARE_COLS], F32, name="shared")
+        total = sb.tile([P, I], F32, name="total")
+        nc.vector.scalar_tensor_tensor(out=own[:, halves[0]], in0=r[:, halves[0]], scalar=2.0, in1=v[:, halves[0]], op0=ALU.subtract, op1=ALU.mult)
+        nc.vector.tensor_tensor(shared[:].indirect(links[:]), v[:], r[:], ALU.mult)
+        nc.vector.scalar_tensor_tensor(out=weighed[:], in0=v[:], scalar=1.0, in1=share[:], op0=ALU.mult, op1=ALU.mult, accum_out=through_z[:])
+        nc.vector.scalar_tensor_tensor(out=own[:, halves[1]], in0=r[:, halves[1]], scalar=2.0, in1=v[:, halves[1]], op0=ALU.subtract, op1=ALU.mult)
+        nc.vector.scalar_tensor_tensor(out=total[:], in0=shared[:, :I], scalar=through_z[:], in1=own[:], op0=ALU.add, op1=ALU.add)
+        nc.vector.tensor_tensor(gf[:].indirect(tokens[:]), total[:], share[:], ALU.mult)
+
+        start = 0
+        for n, width in enumerate(OUT_CHUNKS):
+            cols = slice(start, start + width)
+            summed = sb.tile([P, width], F32, name="summed%d" % n)
+            nc.vector.tensor_tensor(out=summed[:], in0=gf[:, cols], in1=before[:, cols], op=ALU.add)
+            nc.sync.dma_start(out=out[:, cols], in_=summed[:])
+            start = start + width

@@ -21,7 +21,7 @@ H = I // 2
 LIST_COLS = I // 16
 SHARE_COLS = 768
 VAL_PLANE = 4
-OUT_CHUNKS = (512, 512, 512, 256, 256)
+OUT_CHUNKS = (256, 512, 512, 512, 256)
 
 
 def tile_attend_bneighbourshare_s_kernel(tc, query, keys_words, keys_scales, reserve, gout, vals_words, vals_scales, old, offs2, offs, out):
@@ -29,6 +29,7 @@ def tile_attend_bneighbourshare_s_kernel(tc, query, keys_words, keys_scales, res
     with ExitStack() as ctx:
         lists = ctx.enter_context(tc.tile_pool(name="lists", bufs=1))
         sb = ctx.enter_context(tc.tile_pool(name="sb", bufs=1))
+        placed = ctx.enter_context(tc.tile_pool(name="placed", bufs=1))
         psum = ctx.enter_context(tc.psum_pool(name="psum", bufs=1))
 
         halves = [slice(h * H, (h + 1) * H) for h in range(2)]
@@ -39,24 +40,24 @@ def tile_attend_bneighbourshare_s_kernel(tc, query, keys_words, keys_scales, res
         nc.sync.dma_start(tokens[:], offs)
         nc.sync.dma_start(links[:], offs2)
 
-        q_raw = sb.tile([P, PACK, Q], F32, name="q_raw", tag="staged", align_bytes=64)
+        q_raw = sb.tile([P, PACK, Q], F32, name="q_raw", tag="query_values_r", align_bytes=64)
         nc.scalar.dma_start(out=q_raw[:], in_=query.rearrange("(p j) w -> p j w", j=PACK))
-        k_pool = sb.tile([P, T], I32, name="k_pool", tag="keys_then_scales", align_bytes=64)
+        k_pool = sb.tile([P, T], I32, name="k_pool", tag="keys_scales_old", align_bytes=64)
         nc.scalar.dma_start(out=k_pool[:], in_=keys_words[0].rearrange("p n t -> p (n t)").bitcast(I32))
-        g_raw = sb.tile([P, PACK, Q], F32, name="g_raw", align_bytes=64)
+        g_raw = sb.tile([P, PACK, Q], F32, name="g_raw", tag="gout_p", align_bytes=64)
         nc.scalar.dma_start(out=g_raw[:], in_=gout.rearrange("(p j) w -> p j w", j=PACK))
 
-        def load_scales(name, scales, first, queues):
-            plane = sb.tile([P, T], U8, name=name, align_bytes=64)
+        def load_scales(plane, scales, first, queues):
             words = plane[:].bitcast(I32)
             nc.vector.memset(words, 0)
             rows = scales[0].bitcast(I32)
             for quad in range(4):
                 queues[quad].dma_start(out=words[32 * quad + first : 32 * quad + first + 4, :], in_=rows[4 * quad : 4 * quad + 4, :])
-            return plane
 
-        ks_pool = load_scales("ks_pool", keys_scales, 0, [nc.sync] * 4)
-        vs_pool = load_scales("vs_pool", vals_scales, VAL_PLANE, [nc.gpsimd, nc.gpsimd, nc.sync, nc.sync])
+        ks_pool = sb.tile([P, T], U8, name="ks_pool", align_bytes=64)
+        vs_pool = placed.tile([P, T], U8, name="vs_pool", align_bytes=64, offset=0)
+        load_scales(ks_pool, keys_scales, 0, [nc.sync] * 4)
+        load_scales(vs_pool, vals_scales, VAL_PLANE, [nc.gpsimd] * 3 + [nc.sync])
         res = sb.tile([P, 1], F32, name="res")
         nc.gpsimd.dma_start(out=res[:], in_=reserve)
 
@@ -69,84 +70,89 @@ def tile_attend_bneighbourshare_s_kernel(tc, query, keys_words, keys_scales, res
             nc.scalar.copy(out=grouped[:], in_=raw[:].rearrange("p j w -> p w j"))
             return grouped
 
-        def quantize(name, grouped):
-            codes = sb.tile([P, Q], U32, name=name + "_codes", align_bytes=64)
+        def quantize(name, grouped, codes):
             scales = sb.tile([P, Q], U8, name=name + "_scales", align_bytes=64)
             nc.vector.quantize_mx(out=codes[:].bitcast(FP8X4), scales=scales[:], in_=grouped[:].rearrange("p w j -> p (w j)"))
-            return codes, scales
+            return scales
 
         def gather_scales(name, plane, tag):
             picked = sb.tile([P, I], U8, name=name, tag=tag, align_bytes=64)
             nc.vector.tensor_copy(picked[:], plane[:].indirect(tokens[:]))
             return picked
 
-        def products(name, pool_words, picked_scales, first, codes, scales):
+        def products(name, pool_words, picked_scales, first, codes, scales, tag):
             banks = []
+            picked = sb.tile([P, I], U32, name=name + "_words", tag=tag, align_bytes=64)
             for h in range(2):
-                picked = sb.tile([P, H], U32, name=name + "_words%d" % h, align_bytes=64)
-                nc.vector.tensor_copy(picked[:], pool_words[:].bitcast(U32).indirect(tokens[:, list_halves[h]]))
+                nc.vector.tensor_copy(picked[:, halves[h]], pool_words[:].bitcast(U32).indirect(tokens[:, list_halves[h]]))
                 bank = psum.tile([P, H], F32, name=name + "_bank%d" % h)
                 nc.tensor.matmul_mx(
                     out=bank[:], lhsT=codes[:].bitcast(FP8X4), lhsT_scale=scales[:],
-                    rhs=picked[:].bitcast(FP8X4), rhs_scale=picked_scales[first:P, halves[h]],
+                    rhs=picked[:, halves[h]].bitcast(FP8X4), rhs_scale=picked_scales[first:P, halves[h]],
                     start=True, stop=True,
                 )
                 banks.append(bank)
             return banks
 
         q_grouped = interleave("q_grouped", q_raw)
-        v_pool = sb.tile([P, T], I32, name="v_pool", tag="staged", align_bytes=64)
+        v_pool = sb.tile([P, T], I32, name="v_pool", tag="query_values_r", align_bytes=64)
         nc.scalar.dma_start(out=v_pool[:], in_=vals_words[0].rearrange("p n t -> p (n t)").bitcast(I32))
+        g_grouped = interleave("g_grouped", g_raw)
         ks = gather_scales("ks", ks_pool, "ks")
-        q_codes, q_scales = quantize("q", q_grouped)
-        a = products("a", k_pool, ks, 0, q_codes, q_scales)
+        q_codes = sb.tile([P, Q], U32, name="q_codes", align_bytes=64)
+        q_scales = quantize("q", q_grouped, q_codes)
+        a = products("a", k_pool, ks, 0, q_codes, q_scales, "k_picked")
 
-        p = sb.tile([P, I], F32, name="p")
+        p = sb.tile([P, I], F32, name="p", tag="gout_p", align_bytes=64)
+        p_again = sb.tile([P, I], F32, name="p_again", tag="p_again_values", align_bytes=64)
         z_part = [sb.tile([P, 1], F32, name="z_part%d" % h) for h in range(2)]
         for h in range(2):
-            nc.scalar.activation(out=p[:, halves[h]], in_=a[h][:], func=ACT.Exp, accum_out=z_part[h][:])
-        g_grouped = interleave("g_grouped", g_raw)
-        vs = gather_scales("vs", vs_pool, "keys_then_scales")
+            nc.scalar.activation(out=p[:, halves[h]], in_=a[h][:], func=ACT.Exp)
+            nc.scalar.activation(out=p_again[:, halves[h]], in_=a[h][:], func=ACT.Exp, accum_out=z_part[h][:])
+        vs = gather_scales("vs", vs_pool, "keys_scales_old")
 
-        linked = sb.tile([P, I], F32, name="linked")
-        den = sb.tile([P, I], F32, name="den")
+        g_codes = placed.tile([P, Q], U32, name="g_codes", align_bytes=64, offset=0)
+        pair = placed.tile([P, I], F32, name="pair", align_bytes=64, offset=4 * Q)
         root = sb.tile([P, I], F32, name="root")
         inv = sb.tile([P, I], F32, name="inv")
-        for h in range(2):
-            nc.vector.tensor_copy(linked[:, halves[h]], p[:].indirect(links[:, list_halves[h]]))
-        for h in range(2):
-            nc.vector.scalar_tensor_tensor(out=den[:, halves[h]], in0=linked[:, halves[h]], scalar=res[:], in1=p[:, halves[h]], op0=ALU.add, op1=ALU.add)
-            nc.scalar.activation(out=root[:, halves[h]], in_=den[:, halves[h]], func=ACT.Abs_reciprocal_sqrt)
-            nc.scalar.activation(out=inv[:, halves[h]], in_=root[:, halves[h]], func=ACT.Square)
         z_root = sb.tile([P, 1], F32, name="z_root")
         z_inv = sb.tile([P, 1], F32, name="z_inv")
-        share = sb.tile([P, I], F32, name="share")
+        g_scales = quantize("g", g_grouped, g_codes)
+        for h in range(2):
+            nc.vector.tensor_tensor(pair[:, halves[h]], p[:].indirect(links[:, list_halves[h]]), p_again[:, halves[h]], ALU.add)
         nc.scalar.activation(out=z_root[:], in_=z_part[0][:], func=ACT.Abs_reciprocal_sqrt, bias=z_part[1][:])
         nc.scalar.activation(out=z_inv[:], in_=z_root[:], func=ACT.Square)
-        nc.scalar.activation(out=share[:], in_=p[:], func=ACT.Copy, scale=z_inv[:])
+        for h in range(2):
+            nc.scalar.activation(out=root[:, halves[h]], in_=pair[:, halves[h]], func=ACT.Abs_reciprocal_sqrt, bias=res[:])
+        for h in range(2):
+            nc.scalar.activation(out=inv[:, halves[h]], in_=root[:, halves[h]], func=ACT.Square)
 
-        g_codes, g_scales = quantize("g", g_grouped)
-        c0 = products("c0", v_pool, vs, VAL_PLANE, g_codes, g_scales)
-        before = sb.tile([P, T], F32, name="before", tag="staged", align_bytes=64)
+        c0 = products("c0", v_pool, vs, VAL_PLANE, g_codes, g_scales, "p_again_values")
+        before = sb.tile([P, T], F32, name="before", tag="keys_scales_old", align_bytes=64)
         nc.sync.dma_start(out=before[:], in_=old)
 
-        r = sb.tile([P, I], F32, name="r")
-        v = sb.tile([P, I], F32, name="v")
+        dr = sb.tile([P, I], F32, name="dr")
+        r = sb.tile([P, I], F32, name="r", tag="query_values_r", align_bytes=64)
+        w = sb.tile([P, I], F32, name="w")
+        w_part = [sb.tile([P, 1], F32, name="w_part%d" % h) for h in range(2)]
+        own = sb.tile([P, I], F32, name="own")
+        shared = sb.tile([P, SHARE_COLS], F32, name="shared")
+        rest = sb.tile([P, I], F32, name="rest")
+        dz_part = sb.tile([P, 1], F32, name="dz_part")
+        dz = sb.tile([P, 1], F32, name="dz")
+        for h in range(2):
+            nc.vector.scalar_tensor_tensor(out=dr[:, halves[h]], in0=c0[h][:], scalar=z_inv[:], in1=p[:, halves[h]], op0=ALU.mult, op1=ALU.mult)
         for h in range(2):
             nc.vector.tensor_tensor(out=r[:, halves[h]], in0=p[:, halves[h]], in1=inv[:, halves[h]], op=ALU.mult)
         for h in range(2):
-            nc.vector.scalar_tensor_tensor(out=v[:, halves[h]], in0=c0[h][:], scalar=-512.0, in1=r[:, halves[h]], op0=ALU.mult, op1=ALU.mult)
-        weighed = sb.tile([P, I], F32, name="weighed")
-        through_z = sb.tile([P, 1], F32, name="through_z")
-        own = sb.tile([P, I], F32, name="own")
-        shared = sb.tile([P, SHARE_COLS], F32, name="shared")
-        total = sb.tile([P, I], F32, name="total")
-        nc.vector.scalar_tensor_tensor(out=own[:, halves[0]], in0=r[:, halves[0]], scalar=2.0, in1=v[:, halves[0]], op0=ALU.subtract, op1=ALU.mult)
-        nc.vector.tensor_tensor(shared[:].indirect(links[:]), v[:], r[:], ALU.mult)
-        nc.vector.scalar_tensor_tensor(out=weighed[:], in0=v[:], scalar=1.0, in1=share[:], op0=ALU.mult, op1=ALU.mult, accum_out=through_z[:])
-        nc.vector.scalar_tensor_tensor(out=own[:, halves[1]], in0=r[:, halves[1]], scalar=2.0, in1=v[:, halves[1]], op0=ALU.subtract, op1=ALU.mult)
-        nc.vector.scalar_tensor_tensor(out=total[:], in0=shared[:, :I], scalar=through_z[:], in1=own[:], op0=ALU.add, op1=ALU.add)
-        nc.vector.tensor_tensor(gf[:].indirect(tokens[:]), total[:], share[:], ALU.mult)
+            nc.vector.scalar_tensor_tensor(out=w[:, halves[h]], in0=dr[:, halves[h]], scalar=-512.0, in1=r[:, halves[h]], op0=ALU.mult, op1=ALU.mult, accum_out=w_part[h][:])
+        nc.scalar.activation(out=dz_part[:], in_=w_part[0][:], func=ACT.Copy, scale=z_inv[:])
+        nc.scalar.activation(out=dz[:], in_=w_part[1][:], func=ACT.Identity, scale=z_inv[:], bias=dz_part[:])
+        nc.vector.scalar_tensor_tensor(out=own[:, halves[0]], in0=r[:, halves[0]], scalar=2.0, in1=w[:, halves[0]], op0=ALU.subtract, op1=ALU.mult)
+        nc.vector.tensor_tensor(shared[:].indirect(links[:]), w[:], inv[:], ALU.mult)
+        nc.vector.scalar_tensor_tensor(out=own[:, halves[1]], in0=r[:, halves[1]], scalar=2.0, in1=w[:, halves[1]], op0=ALU.subtract, op1=ALU.mult)
+        nc.vector.scalar_tensor_tensor(out=rest[:], in0=shared[:, :I], scalar=dz[:], in1=p[:], op0=ALU.add, op1=ALU.mult)
+        nc.vector.tensor_tensor(gf[:].indirect(tokens[:]), rest[:], own[:], ALU.add)
 
         start = 0
         for n, width in enumerate(OUT_CHUNKS):

@@ -29,41 +29,40 @@ def tile_attend_bneighbourshare_s_kernel(tc, query, keys_words, keys_scales, res
     with ExitStack() as ctx:
         lists = ctx.enter_context(tc.tile_pool(name="lists", bufs=1))
         sb = ctx.enter_context(tc.tile_pool(name="sb", bufs=1))
-        placed = ctx.enter_context(tc.tile_pool(name="placed", bufs=1))
         psum = ctx.enter_context(tc.psum_pool(name="psum", bufs=1))
 
         halves = [slice(h * H, (h + 1) * H) for h in range(2)]
         list_halves = [slice(h * LIST_COLS // 2, (h + 1) * LIST_COLS // 2) for h in range(2)]
 
+        def load_scales(plane, scales, first):
+            words = plane[:].bitcast(I32)
+            rows = scales[0].bitcast(I32)
+            for quad in range(4):
+                nc.sync.dma_start(out=words[32 * quad + first : 32 * quad + first + 4, :], in_=rows[4 * quad : 4 * quad + 4, :])
+
+        ks_pool = sb.tile([P, T], U8, name="ks_pool", align_bytes=64)
+        vs_pool = sb.tile([P, T], U8, name="vs_pool", tag="scales_pair", align_bytes=64)
+        gf = sb.tile([P, T], F32, name="gf")
+        nc.vector.memset(ks_pool[:].bitcast(I32), 0)
+        nc.vector.memset(vs_pool[:].bitcast(I32), 0)
+        nc.vector.memset(gf[:], 0.0)
+
+        q_raw = sb.tile([P, PACK, Q], F32, name="q_raw", align_bytes=64)
+        nc.sync.dma_start(out=q_raw[:], in_=query.rearrange("(p j) w -> p j w", j=PACK))
         tokens = lists.tile([P, LIST_COLS], U16, name="tokens")
         links = lists.tile([P, LIST_COLS], U16, name="links")
         nc.sync.dma_start(tokens[:], offs)
         nc.sync.dma_start(links[:], offs2)
-
-        q_raw = sb.tile([P, PACK, Q], F32, name="q_raw", tag="query_values_r", align_bytes=64)
-        nc.scalar.dma_start(out=q_raw[:], in_=query.rearrange("(p j) w -> p j w", j=PACK))
-        k_pool = sb.tile([P, T], I32, name="k_pool", tag="keys_scales_old", align_bytes=64)
-        nc.scalar.dma_start(out=k_pool[:], in_=keys_words[0].rearrange("p n t -> p (n t)").bitcast(I32))
+        load_scales(ks_pool, keys_scales, 0)
+        k_pool = sb.tile([P, T], I32, name="k_pool", tag="keys_old", align_bytes=64)
+        nc.sync.dma_start(out=k_pool[:], in_=keys_words[0].rearrange("p n t -> p (n t)").bitcast(I32))
         g_raw = sb.tile([P, PACK, Q], F32, name="g_raw", tag="gout_p", align_bytes=64)
-        nc.scalar.dma_start(out=g_raw[:], in_=gout.rearrange("(p j) w -> p j w", j=PACK))
-
-        def load_scales(plane, scales, first, queues):
-            words = plane[:].bitcast(I32)
-            nc.vector.memset(words, 0)
-            rows = scales[0].bitcast(I32)
-            for quad in range(4):
-                queues[quad].dma_start(out=words[32 * quad + first : 32 * quad + first + 4, :], in_=rows[4 * quad : 4 * quad + 4, :])
-
-        ks_pool = sb.tile([P, T], U8, name="ks_pool", align_bytes=64)
-        vs_pool = placed.tile([P, T], U8, name="vs_pool", align_bytes=64, offset=0)
-        load_scales(ks_pool, keys_scales, 0, [nc.sync] * 4)
-        load_scales(vs_pool, vals_scales, VAL_PLANE, [nc.gpsimd] * 3 + [nc.sync])
+        nc.sync.dma_start(out=g_raw[:], in_=gout.rearrange("(p j) w -> p j w", j=PACK))
+        load_scales(vs_pool, vals_scales, VAL_PLANE)
+        v_pool = sb.tile([P, T], I32, name="v_pool", tag="values_r", align_bytes=64)
+        nc.sync.dma_start(out=v_pool[:], in_=vals_words[0].rearrange("p n t -> p (n t)").bitcast(I32))
         res = sb.tile([P, 1], F32, name="res")
-        nc.gpsimd.dma_start(out=res[:], in_=reserve)
-
-        gf = sb.tile([P, T], F32, name="gf")
-        nc.vector.memset(gf[:, : T // 2 + 1], 0.0)
-        nc.vector.memset(gf[:, T // 2 + 1 :], 0.0)
+        nc.sync.dma_start(out=res[:], in_=reserve)
 
         def interleave(name, raw):
             grouped = sb.tile([P, Q, PACK], BF16, name=name, align_bytes=64)
@@ -95,8 +94,6 @@ def tile_attend_bneighbourshare_s_kernel(tc, query, keys_words, keys_scales, res
             return banks
 
         q_grouped = interleave("q_grouped", q_raw)
-        v_pool = sb.tile([P, T], I32, name="v_pool", tag="query_values_r", align_bytes=64)
-        nc.scalar.dma_start(out=v_pool[:], in_=vals_words[0].rearrange("p n t -> p (n t)").bitcast(I32))
         g_grouped = interleave("g_grouped", g_raw)
         ks = gather_scales("ks", ks_pool, "ks")
         q_codes = sb.tile([P, Q], U32, name="q_codes", align_bytes=64)
@@ -104,22 +101,20 @@ def tile_attend_bneighbourshare_s_kernel(tc, query, keys_words, keys_scales, res
         a = products("a", k_pool, ks, 0, q_codes, q_scales, "k_picked")
 
         p = sb.tile([P, I], F32, name="p", tag="gout_p", align_bytes=64)
-        p_again = sb.tile([P, I], F32, name="p_again", tag="p_again_values", align_bytes=64)
+        p_again = [sb.tile([P, H], F32, name="p_again%d" % h, tag=("p_again_codes", "p_again_values")[h], align_bytes=64) for h in range(2)]
         z_part = [sb.tile([P, 1], F32, name="z_part%d" % h) for h in range(2)]
         for h in range(2):
             nc.scalar.activation(out=p[:, halves[h]], in_=a[h][:], func=ACT.Exp)
-            nc.scalar.activation(out=p_again[:, halves[h]], in_=a[h][:], func=ACT.Exp, accum_out=z_part[h][:])
-        vs = gather_scales("vs", vs_pool, "keys_scales_old")
+            nc.scalar.activation(out=p_again[h][:], in_=a[h][:], func=ACT.Exp, accum_out=z_part[h][:])
+        vs = gather_scales("vs", vs_pool, "vs")
 
-        g_codes = placed.tile([P, Q], U32, name="g_codes", align_bytes=64, offset=0)
-        pair = placed.tile([P, I], F32, name="pair", align_bytes=64, offset=4 * Q)
+        pair = sb.tile([P, I], F32, name="pair", tag="scales_pair", align_bytes=64)
         root = sb.tile([P, I], F32, name="root")
         inv = sb.tile([P, I], F32, name="inv")
         z_root = sb.tile([P, 1], F32, name="z_root")
         z_inv = sb.tile([P, 1], F32, name="z_inv")
-        g_scales = quantize("g", g_grouped, g_codes)
         for h in range(2):
-            nc.vector.tensor_tensor(pair[:, halves[h]], p[:].indirect(links[:, list_halves[h]]), p_again[:, halves[h]], ALU.add)
+            nc.vector.tensor_tensor(pair[:, halves[h]], p[:].indirect(links[:, list_halves[h]]), p_again[h][:], ALU.add)
         nc.scalar.activation(out=z_root[:], in_=z_part[0][:], func=ACT.Abs_reciprocal_sqrt, bias=z_part[1][:])
         nc.scalar.activation(out=z_inv[:], in_=z_root[:], func=ACT.Square)
         for h in range(2):
@@ -127,12 +122,14 @@ def tile_attend_bneighbourshare_s_kernel(tc, query, keys_words, keys_scales, res
         for h in range(2):
             nc.scalar.activation(out=inv[:, halves[h]], in_=root[:, halves[h]], func=ACT.Square)
 
+        g_codes = sb.tile([P, Q], U32, name="g_codes", tag="p_again_codes", align_bytes=64)
+        g_scales = quantize("g", g_grouped, g_codes)
         c0 = products("c0", v_pool, vs, VAL_PLANE, g_codes, g_scales, "p_again_values")
-        before = sb.tile([P, T], F32, name="before", tag="keys_scales_old", align_bytes=64)
+        before = sb.tile([P, T], F32, name="before", tag="keys_old", align_bytes=64)
         nc.sync.dma_start(out=before[:], in_=old)
 
         dr = sb.tile([P, I], F32, name="dr")
-        r = sb.tile([P, I], F32, name="r", tag="query_values_r", align_bytes=64)
+        r = sb.tile([P, I], F32, name="r", tag="values_r", align_bytes=64)
         w = sb.tile([P, I], F32, name="w")
         w_part = [sb.tile([P, 1], F32, name="w_part%d" % h) for h in range(2)]
         own = sb.tile([P, I], F32, name="own")

from contextlib import ExitStack

import concourse.mybir as mybir

D, E, T, I, Q = 512, 512, 2048, 512, 128
FLOPS = 2 * Q * I * (D + E)

F32 = mybir.dt.float32
BF16 = mybir.dt.bfloat16
I32 = mybir.dt.int32
U32 = mybir.dt.uint32
U16 = mybir.dt.uint16
U8 = mybir.dt.uint8
FP8X4 = mybir.dt.float8_e4m3fn_x4
ALU = mybir.AluOpType
ACT = mybir.ActivationFunctionType

P = 128
PACK = 4
H = I // 2
LIST_COLS = I // 16
SHARE_COLS = 768
VAL_PLANE = 4
OUT_CHUNKS = (256, 512, 512, 512, 256)


def tile_attend_bneighbourshare_s_kernel(tc, query, keys_words, keys_scales, reserve, gout, vals_words, vals_scales, old, offs2, offs, out):
    nc = tc.nc
    with ExitStack() as ctx:
        lists = ctx.enter_context(tc.tile_pool(name="lists", bufs=1))
        sb = ctx.enter_context(tc.tile_pool(name="sb", bufs=1))
        psum = ctx.enter_context(tc.psum_pool(name="psum", bufs=1))

        halves = [slice(h * H, (h + 1) * H) for h in range(2)]
        list_halves = [slice(h * LIST_COLS // 2, (h + 1) * LIST_COLS // 2) for h in range(2)]

        def load_scales(plane, scales, first):
            words = plane[:].bitcast(I32)
            rows = scales[0].bitcast(I32)
            for quad in range(4):
                nc.sync.dma_start(out=words[32 * quad + first : 32 * quad + first + 4, :], in_=rows[4 * quad : 4 * quad + 4, :])

        ks_pool = sb.tile([P, T], U8, name="ks_pool", align_bytes=64)
        vs_pool = sb.tile([P, T], U8, name="vs_pool", tag="scales_pair", align_bytes=64)
        gf = sb.tile([P, T], F32, name="gf")
        nc.vector.memset(ks_pool[:].bitcast(I32), 0)
        nc.vector.memset(vs_pool[:].bitcast(I32), 0)
        nc.vector.memset(gf[:], 0.0)

        q_raw = sb.tile([P, PACK, Q], F32, name="q_raw", align_bytes=64)
        nc.sync.dma_start(out=q_raw[:], in_=query.rearrange("(p j) w -> p j w", j=PACK))
        tokens = lists.tile([P, LIST_COLS], U16, name="tokens")
        links = lists.tile([P, LIST_COLS], U16, name="links")
        nc.sync.dma_start(tokens[:], offs)
        nc.sync.dma_start(links[:], offs2)
        load_scales(ks_pool, keys_scales, 0)
        k_pool = sb.tile([P, T], I32, name="k_pool", tag="keys_old", align_bytes=64)
        nc.sync.dma_start(out=k_pool[:], in_=keys_words[0].rearrange("p n t -> p (n t)").bitcast(I32))
        g_raw = sb.tile([P, PACK, Q], F32, name="g_raw", tag="gout_p", align_bytes=64)
        nc.sync.dma_start(out=g_raw[:], in_=gout.rearrange("(p j) w -> p j w", j=PACK))
        load_scales(vs_pool, vals_scales, VAL_PLANE)
        v_pool = sb.tile([P, T], I32, name="v_pool", tag="values_r", align_bytes=64)
        nc.sync.dma_start(out=v_pool[:], in_=vals_words[0].rearrange("p n t -> p (n t)").bitcast(I32))
        res = sb.tile([P, 1], F32, name="res")
        nc.sync.dma_start(out=res[:], in_=reserve)

        def interleave(name, raw):
            grouped = sb.tile([P, Q, PACK], BF16, name=name, align_bytes=64)
            nc.scalar.copy(out=grouped[:], in_=raw[:].rearrange("p j w -> p w j"))
            return grouped

        def quantize(name, grouped, codes):
            scales = sb.tile([P, Q], U8, name=name + "_scales", align_bytes=64)
            nc.vector.quantize_mx(out=codes[:].bitcast(FP8X4), scales=scales[:], in_=grouped[:].rearrange("p w j -> p (w j)"))
            return scales

        def gather_scales(name, plane, tag):
            picked = sb.tile([P, I], U8, name=name, tag=tag, align_bytes=64)
            nc.vector.tensor_copy(picked[:], plane[:].indirect(tokens[:]))
            return picked

        def products(name, pool_words, picked_scales, first, codes, scales, tag):
            banks = []
            picked = sb.tile([P, I], U32, name=name + "_words", tag=tag, align_bytes=64)
            for h in range(2):
                nc.vector.tensor_copy(picked[:, halves[h]], pool_words[:].bitcast(U32).indirect(tokens[:, list_halves[h]]))
                bank = psum.tile([P, H], F32, name=name + "_bank%d" % h)
                nc.tensor.matmul_mx(
                    out=bank[:], lhsT=codes[:].bitcast(FP8X4), lhsT_scale=scales[:],
                    rhs=picked[:, halves[h]].bitcast(FP8X4), rhs_scale=picked_scales[first:P, halves[h]],
                    start=True, stop=True,
                )
                banks.append(bank)
            return banks

        q_grouped = interleave("q_grouped", q_raw)
        g_grouped = interleave("g_grouped", g_raw)
        ks = gather_scales("ks", ks_pool, "ks")
        q_codes = sb.tile([P, Q], U32, name="q_codes", align_bytes=64)
        q_scales = quantize("q", q_grouped, q_codes)
        a = products("a", k_pool, ks, 0, q_codes, q_scales, "k_picked")

        p = sb.tile([P, I], F32, name="p", tag="gout_p", align_bytes=64)
        p_again = [sb.tile([P, H], F32, name="p_again%d" % h, tag=("p_again_codes", "p_again_values")[h], align_bytes=64) for h in range(2)]
        z_part = [sb.tile([P, 1], F32, name="z_part%d" % h) for h in range(2)]
        for h in range(2):
            nc.scalar.activation(out=p[:, halves[h]], in_=a[h][:], func=ACT.Exp)
            nc.scalar.activation(out=p_again[h][:], in_=a[h][:], func=ACT.Exp, accum_out=z_part[h][:])
        vs = gather_scales("vs", vs_pool, "vs")

        pair = sb.tile([P, I], F32, name="pair", tag="scales_pair", align_bytes=64)
        root = sb.tile([P, I], F32, name="root")
        inv = sb.tile([P, I], F32, name="inv")
        z_root = sb.tile([P, 1], F32, name="z_root")
        z_inv = sb.tile([P, 1], F32, name="z_inv")
        for h in range(2):
            nc.vector.tensor_tensor(pair[:, halves[h]], p[:].indirect(links[:, list_halves[h]]), p_again[h][:], ALU.add)
        nc.scalar.activation(out=z_root[:], in_=z_part[0][:], func=ACT.Abs_reciprocal_sqrt, bias=z_part[1][:])
        nc.scalar.activation(out=z_inv[:], in_=z_root[:], func=ACT.Square)
        for h in range(2):
            nc.scalar.activation(out=root[:, halves[h]], in_=pair[:, halves[h]], func=ACT.Abs_reciprocal_sqrt, bias=res[:])
        for h in range(2):
            nc.scalar.activation(out=inv[:, halves[h]], in_=root[:, halves[h]], func=ACT.Square)

        g_codes = sb.tile([P, Q], U32, name="g_codes", tag="p_again_codes", align_bytes=64)
        g_scales = quantize("g", g_grouped, g_codes)
        c0 = products("c0", v_pool, vs, VAL_PLANE, g_codes, g_scales, "p_again_values")
        before = sb.tile([P, T], F32, name="before", tag="keys_old", align_bytes=64)
        nc.sync.dma_start(out=before[:], in_=old)

        dr = sb.tile([P, I], F32, name="dr")
        r = sb.tile([P, I], F32, name="r", tag="values_r", align_bytes=64)
        w = sb.tile([P, I], F32, name="w")
        w_part = [sb.tile([P, 1], F32, name="w_part%d" % h) for h in range(2)]
        own = sb.tile([P, I], F32, name="own")
        shared = sb.tile([P, SHARE_COLS], F32, name="shared")
        rest = sb.tile([P, I], F32, name="rest")
        dz_part = sb.tile([P, 1], F32, name="dz_part")
        dz = sb.tile([P, 1], F32, name="dz")
        for h in range(2):
            nc.vector.scalar_tensor_tensor(out=dr[:, halves[h]], in0=c0[h][:], scalar=z_inv[:], in1=p[:, halves[h]], op0=ALU.mult, op1=ALU.mult)
        for h in range(2):
            nc.vector.tensor_tensor(out=r[:, halves[h]], in0=p[:, halves[h]], in1=inv[:, halves[h]], op=ALU.mult)
        for h in range(2):
            nc.vector.scalar_tensor_tensor(out=w[:, halves[h]], in0=dr[:, halves[h]], scalar=-512.0, in1=r[:, halves[h]], op0=ALU.mult, op1=ALU.mult, accum_out=w_part[h][:])
        nc.scalar.activation(out=dz_part[:], in_=w_part[0][:], func=ACT.Copy, scale=z_inv[:])
        nc.scalar.activation(out=dz[:], in_=w_part[1][:], func=ACT.Identity, scale=z_inv[:], bias=dz_part[:])
        nc.vector.scalar_tensor_tensor(out=own[:, halves[0]], in0=r[:, halves[0]], scalar=2.0, in1=w[:, halves[0]], op0=ALU.subtract, op1=ALU.mult)
        nc.vector.tensor_tensor(shared[:].indirect(links[:]), w[:], inv[:], ALU.mult)
        nc.vector.scalar_tensor_tensor(out=own[:, halves[1]], in0=r[:, halves[1]], scalar=2.0, in1=w[:, halves[1]], op0=ALU.subtract, op1=ALU.mult)
        nc.vector.scalar_tensor_tensor(out=rest[:], in0=shared[:, :I], scalar=dz[:], in1=p[:], op0=ALU.add, op1=ALU.mult)
        nc.vector.tensor_tensor(gf[:].indirect(tokens[:]), rest[:], own[:], ALU.add)

        start = 0
        for n, width in enumerate(OUT_CHUNKS):
            cols = slice(start, start + width)
            summed = sb.tile([P, width], F32, name="summed%d" % n)
            nc.vector.tensor_tensor(out=summed[:], in0=gf[:, cols], in1=before[:, cols], op=ALU.add)
            nc.sync.dma_start(out=out[:, cols], in_=summed[:])
            start = start + width
